import numpy as np
import ml_dtypes


def mxq(x, axis, fmt="e4m3"):
    dtype, down = {"e4m3": (ml_dtypes.float8_e4m3fn, 7), "e5m2": (ml_dtypes.float8_e5m2, 14)}[fmt]
    v = np.moveaxis(np.asarray(x, np.float32).astype(ml_dtypes.bfloat16).astype(np.float64), axis, -1)
    blocks = v.reshape(v.shape[:-1] + (-1, 32))
    amax = np.abs(blocks).max(-1, keepdims=True)
    byte = np.maximum(np.where(amax > 0, np.frexp(amax)[1] - 1 + 127, 0) - down, 1)
    scale = np.exp2(byte - 127.0)
    codes = (blocks / scale).astype(np.float32).astype(dtype).astype(np.float64)
    return np.moveaxis((codes * scale).reshape(v.shape), -1, axis)


WIDE = False


def mx_kscale(k):
    if not WIDE:
        return np.ones(k)
    levels = np.array([10, -10, 5, -5, 0])
    if k % 512:
        return np.exp2(np.random.permutation(np.resize(levels, k // 32))).repeat(32)
    a = np.empty((k // 512, 16))
    for p in range(k // 512):
        a[p, :8] = np.random.permutation(np.resize(levels, 8))
        for g in range(8):
            far = levels[np.abs(levels - a[p, g]) >= 10]
            a[p, g + 8] = far[np.random.randint(len(far))]
    return np.exp2(a.ravel()).repeat(32)


def f64(x):
    return np.asarray(x).astype(np.float64)


def striped(idx):
    return np.tile(idx.reshape(-1, 16).T, (8, 1)).astype(np.uint16)


def unstriped(offs):
    return offs[:16].T.reshape(-1).astype(np.int64)


K, T, E, C, N = 512, 768, 6, 256, 512
M = 512


def by_expert(wq, xq):
    return np.concatenate([wq[e].T @ xq[:, e * C:(e + 1) * C] for e in range(E)], axis=1)


def setup_inputs():
    n = np.random.standard_normal
    s = mx_kscale(K)[:, None]
    v = mx_kscale(N)
    first = np.random.permutation(np.repeat(np.arange(E), T // E))
    second = (first + 1 + np.random.permutation(np.repeat(np.arange(E - 1), -(-T // (E - 1)))[:T])) % E
    while np.bincount(second, minlength=E).max() != T // E:
        load = np.bincount(second, minlength=E); hi, lo = int(load.argmax()), int(load.argmin())
        t = np.flatnonzero((second == hi) & (first != lo))[0]; second[t] = lo
    slot_token = np.empty(E * C, np.int64); pos = np.empty((2, T), np.int64); fill = np.zeros(E, np.int64)
    place = np.stack([np.random.permutation(C) for _ in range(E)])
    for r, deal in enumerate((first, second)):
        for t in np.random.permutation(T):
            e = deal[t]; j = e * C + place[e, fill[e]]; fill[e] += 1; slot_token[j] = t; pos[r, t] = j
    g = np.random.uniform(0.2, 0.8, T)
    return {
        "xT": (n((K, T)) * s).astype(np.float32),
        "w": (n((E, K, N)) / np.sqrt(K) / s[None] * v[None, None, :]).astype(np.float32),
        "wp": (n((N, M)) / np.sqrt(N) / v[:, None]).astype(np.float32),
        "gate": np.stack([np.tile(g, (N, 1)), np.tile(1.0 - g, (N, 1))]).astype(np.float32),
        "offs": striped(slot_token),
        "pos1": striped(pos[0]),
        "pos2": striped(pos[1]),
    }


def reference(xT, w, wp, gate, offs, pos1, pos2):
    idx = unstriped(offs)
    xq = mxq(f64(xT)[:, idx], 0, "e4m3")
    y = by_expert(mxq(f64(w), 1, "e4m3"), xq)
    c = f64(gate[0]) * y[:, unstriped(pos1)] + f64(gate[1]) * y[:, unstriped(pos2)]
    return mxq(f64(wp), 0, "e4m3").T @ mxq(c, 0, "e4m3")

@@ -1,0 +1,214 @@
+from contextlib import ExitStack
+
+import concourse.mybir as mybir
+
+K, T, E, C, N, M = 512, 768, 6, 256, 512, 512
+SLOTS = E * C
+P = 128
+PACK = 4
+
+F32 = mybir.dt.float32
+BF16 = mybir.dt.bfloat16
+I32 = mybir.dt.int32
+U32 = mybir.dt.uint32
+U16 = mybir.dt.uint16
+U8 = mybir.dt.uint8
+FP8X4 = mybir.dt.float8_e4m3fn_x4
+MULT = mybir.AluOpType.mult
+ADD = mybir.AluOpType.add
+COPY = mybir.ActivationFunctionType.Copy
+
+FLOPS = 2 * SLOTS * K * N + 2 * T * N * M
+BYTES = 4 * (K * T + E * K * N + N * M + 2 * T + M * T) + 2 * (SLOTS + 2 * T)
+
+SHARES = (128, 128, 128, 64, 32, 48)
+CHUNKS = (512, 256)
+
+
+def tile_moe_nxt_lin_none_kernel(tc, xT, w, wp, gate, offs, pos1, pos2, out):
+    nc = tc.nc
+    with ExitStack() as ctx:
+        lists = ctx.enter_context(tc.tile_pool(name="lists", bufs=1))
+        keep = ctx.enter_context(tc.tile_pool(name="keep", bufs=1))
+        psum = ctx.enter_context(tc.psum_pool(name="psum", bufs=8))
+
+        offs_sb = lists.tile([P, SLOTS // 16], U16, name="offs_sb")
+        pos1_sb = lists.tile([P, T // 16], U16, name="pos1_sb")
+        pos2_sb = lists.tile([P, T // 16], U16, name="pos2_sb")
+
+        x_cuts = [(0, 512), (512, 256)]
+        x_view = xT.rearrange("(p j) t -> p j t", j=PACK)
+        x_raw = [keep.tile([P, PACK, n], F32, name=f"x_raw{i}") for i, (a, n) in enumerate(x_cuts)]
+        x_grp = [keep.tile([P, n, PACK], BF16, align_bytes=64, name=f"x_grp{i}") for i, (a, n) in enumerate(x_cuts)]
+        x_codes = keep.tile([P, T], U32, align_bytes=64, name="x_codes")
+        x_scales = keep.tile([P, T], U8, align_bytes=64, name="x_scales")
+        s_codes = keep.tile([P, SLOTS], U32, align_bytes=64, name="s_codes")
+        s_scales = keep.tile([P, SLOTS], U8, align_bytes=64, name="s_scales")
+        w_raw = [keep.tile([P, PACK, N], F32, name=f"w_raw{e}") for e in range(E)]
+        w_grp = [keep.tile([P, 4, P, PACK], BF16, align_bytes=64, name=f"w_grp{e}") for e in range(E)]
+        w_codes = [keep.tile([P, N], U32, align_bytes=64, name=f"w_codes{e}") for e in range(E)]
+        w_scales = [keep.tile([P, N], U8, align_bytes=64, name=f"w_scales{e}") for e in range(E)]
+        wp_raw = keep.tile([P, PACK, M], F32, name="wp_raw")
+        wp_grp = keep.tile([P, M, PACK], BF16, align_bytes=64, name="wp_grp")
+        wp_codes = keep.tile([P, M], U32, align_bytes=64, name="wp_codes")
+        wp_scales = keep.tile([P, M], U8, align_bytes=64, name="wp_scales")
+        gate_sb = keep.tile([P, 2, T], F32, name="gate_sb")
+        y = [keep.tile([P, SLOTS], F32, name=f"y{r}") for r in range(4)]
+
+        for i, (a, n) in enumerate(x_cuts):
+            nc.sync.dma_start(x_raw[i][:], x_view[:, :, a : a + n])
+            if i == 0:
+                nc.sync.dma_start(offs_sb[:], offs)
+        for e in range(E):
+            nc.sync.dma_start(w_raw[e][:], w[e].rearrange("(p j) n -> p j n", j=PACK))
+        nc.sync.dma_start(pos1_sb[:], pos1)
+        nc.sync.dma_start(pos2_sb[:], pos2)
+        nc.sync.dma_start(gate_sb[:], gate[:, 0:P, :].rearrange("g p t -> p g t"))
+        nc.sync.dma_start(wp_raw[:], wp.rearrange("(p j) m -> p j m", j=PACK))
+
+        nc.gpsimd.memset(x_scales[:], 0)
+
+        def line_view(grouped, raw):
+            return (grouped.rearrange("p (c i) j -> p c j i", i=4), raw.rearrange("p j (c i) -> p c j i", i=4))
+
+        for i, (a, n) in enumerate(x_cuts):
+            h = n // 2
+            o, s = line_view(x_grp[i][:, 0:h, :], x_raw[i][:, :, 0:h])
+            nc.vector.tensor_copy(o, s)
+            o, s = line_view(x_grp[i][:, h:n, :], x_raw[i][:, :, h:n])
+            nc.scalar.activation(o, s, COPY)
+        for i, (a, n) in enumerate(x_cuts):
+            nc.vector.quantize_mx(
+                out=x_codes[:, a : a + n].bitcast(FP8X4),
+                scales=x_scales[:, a : a + n],
+                in_=x_grp[i][:].rearrange("p t j -> p (t j)"),
+            )
+
+        def gather(e):
+            cols = slice(e * C, (e + 2) * C)
+            picks = offs_sb[:, e * C // 16 : (e + 2) * C // 16]
+            nc.vector.tensor_copy(s_codes[:, cols], x_codes[:].indirect(picks))
+            nc.vector.tensor_copy(s_scales[:, cols], x_scales[:].indirect(picks))
+
+        def interleave_w(e):
+            s = SHARES[e]
+            for a, b, copy in ((0, s, nc.scalar.copy), (s, P, nc.vector.tensor_copy)):
+                if a < b:
+                    copy(
+                        w_grp[e][:, :, a:b, :].rearrange("p r m j -> p m j r"),
+                        w_raw[e][:, :, 4 * a : 4 * b].rearrange("p j (m r) -> p m j r", r=4),
+                    )
+
+        def quantise_w(e, cuts):
+            for a in range(0, 4, 4 // cuts):
+                b = a + 4 // cuts
+                nc.vector.quantize_mx(
+                    out=w_codes[e][:, a * P : b * P].bitcast(FP8X4),
+                    scales=w_scales[e][:, a * P : b * P],
+                    in_=w_grp[e][:, a:b, :, :].rearrange("p r m j -> p (r m j)"),
+                )
+
+        def expert(e, bank, col):
+            for r in range(4):
+                nc.tensor.matmul_mx(
+                    out=bank[r][:, col : col + C],
+                    lhsT=w_codes[e][:, r * P : (r + 1) * P].bitcast(FP8X4),
+                    lhsT_scale=w_scales[e][:, r * P : (r + 1) * P],
+                    rhs=s_codes[:, e * C : (e + 1) * C].bitcast(FP8X4),
+                    rhs_scale=s_scales[:, e * C : (e + 1) * C],
+                    start=True,
+                    stop=True,
+                )
+
+        gather(0)
+        for group in ((0, 1), (2, 3), (4,), (5,)):
+            bank = [psum.tile([P, 512], F32, name="bank") for r in range(4)]
+            for i, e in enumerate(group):
+                interleave_w(e)
+                if e % 2 == 0 and e + 2 < E:
+                    gather(e + 2)
+                quantise_w(e, 2 if e == E - 1 else 1)
+                expert(e, bank, i * C)
+            a, n = group[0] * C, len(group) * C
+            for r in range(4):
+                nc.scalar.copy(y[r][:, a : a + n], bank[r][:, 0:n])
+
+        o, s = line_view(wp_grp[:], wp_raw[:])
+        nc.scalar.copy(o, s)
+
+        chunks = [(sum(CHUNKS[:i]), n) for i, n in enumerate(CHUNKS)]
+        n_chunks = len(chunks)
+        parts = [[keep.tile([P, 4, n], F32, name=f"part{q}_{i}") for q in range(2)] for i, (a, n) in enumerate(chunks)]
+        c_grp = [keep.tile([P, n, 4], BF16, align_bytes=64, name=f"c_grp{i}") for i, (a, n) in enumerate(chunks)]
+        c_codes = [keep.tile([P, n], U32, align_bytes=64, name=f"c_codes{i}") for i, (a, n) in enumerate(chunks)]
+        c_scales = [keep.tile([P, n], U8, align_bytes=64, name=f"c_scales{i}") for i, (a, n) in enumerate(chunks)]
+        o_sb = [keep.tile([P, 4, n], F32, name=f"o_sb{i}") for i, (a, n) in enumerate(chunks)]
+        out_view = out.rearrange("(f p) t -> p f t", p=P)
+
+        def combine_gathers(i, rows):
+            a, n = chunks[i]
+            for r in rows:
+                for q, pos in enumerate((pos1_sb, pos2_sb)):
+                    nc.vector.tensor_tensor(
+                        parts[i][q][:, r, :],
+                        y[r][:].indirect(pos[:, a // 16 : (a + n) // 16]),
+                        gate_sb[:, q, a : a + n],
+                        MULT,
+                    )
+
+        def combine_add(i, lo, hi):
+            nc.vector.tensor_tensor(
+                c_grp[i][:, lo:hi, :].rearrange("p (c i) r -> p c r i", i=4),
+                parts[i][0][:, :, lo:hi].rearrange("p r (c i) -> p c r i", i=4),
+                parts[i][1][:, :, lo:hi].rearrange("p r (c i) -> p c r i", i=4),
+                ADD,
+            )
+
+        def quantise_c(i, lo, hi):
+            nc.vector.quantize_mx(
+                out=c_codes[i][:, lo:hi].bitcast(FP8X4),
+                scales=c_scales[i][:, lo:hi],
+                in_=c_grp[i][:, lo:hi, :].rearrange("p t r -> p (t r)"),
+            )
+
+        def project(i, lo, hi, engines):
+            a, n = chunks[i]
+            w_cols = hi - lo
+            for half in range(2):
+                bank = psum.tile([P, 2, w_cols], F32, name="bank")
+                for u in range(2):
+                    f = 2 * half + u
+                    nc.tensor.matmul_mx(
+                        out=bank[:, u, :],
+                        lhsT=wp_codes[:, f * P : (f + 1) * P].bitcast(FP8X4),
+                        lhsT_scale=wp_scales[:, f * P : (f + 1) * P],
+                        rhs=c_codes[i][:, lo:hi].bitcast(FP8X4),
+                        rhs_scale=c_scales[i][:, lo:hi],
+                        start=True,
+                        stop=True,
+                    )
+                engines[half](o_sb[i][:, 2 * half : 2 * half + 2, lo:hi], bank[:])
+            nc.sync.dma_start(out_view[:, :, a + lo : a + hi], o_sb[i][:, :, lo:hi])
+
+        combine_gathers(0, (0, 1, 2, 3))
+        nc.vector.quantize_mx(
+            out=wp_codes[:].bitcast(FP8X4), scales=wp_scales[:], in_=wp_grp[:].rearrange("p m j -> p (m j)")
+        )
+        for i in range(n_chunks):
+            last = i == n_chunks - 1
+            n = chunks[i][1]
+            if last:
+                h = n // 2
+                combine_add(i, 0, h)
+                combine_add(i, h, n)
+                quantise_c(i, 0, h)
+                quantise_c(i, h, n)
+                project(i, 0, h, (nc.scalar.copy, nc.scalar.copy))
+                project(i, h, n, (nc.scalar.copy, nc.vector.tensor_copy))
+            else:
+                combine_gathers(i + 1, (0, 1))
+                combine_add(i, 0, n)
+                combine_gathers(i + 1, (2, 3))
+                quantise_c(i, 0, n)
+                for lo in range(0, n, 256):
+                    project(i, lo, min(lo + 256, n), (nc.scalar.copy, nc.scalar.copy))

@@ -21,7 +21,7 @@ COPY = mybir.ActivationFunctionType.Copy
 FLOPS = 2 * SLOTS * K * N + 2 * T * N * M
 BYTES = 4 * (K * T + E * K * N + N * M + 2 * T + M * T) + 2 * (SLOTS + 2 * T)
 
-SHARES = (128, 128, 128, 64, 32, 48)
+SHARES = (128, 128, 128, 128, 112, 96)
 CHUNKS = (512, 256)
 
 
@@ -30,6 +30,7 @@ def tile_moe_nxt_lin_none_kernel(tc, xT, w, wp, gate, offs, pos1, pos2, out):
     with ExitStack() as ctx:
         lists = ctx.enter_context(tc.tile_pool(name="lists", bufs=1))
         keep = ctx.enter_context(tc.tile_pool(name="keep", bufs=1))
+        slots = ctx.enter_context(tc.tile_pool(name="slots", bufs=2))
         psum = ctx.enter_context(tc.psum_pool(name="psum", bufs=8))
 
         offs_sb = lists.tile([P, SLOTS // 16], U16, name="offs_sb")
@@ -42,8 +43,6 @@ def tile_moe_nxt_lin_none_kernel(tc, xT, w, wp, gate, offs, pos1, pos2, out):
         x_grp = [keep.tile([P, n, PACK], BF16, align_bytes=64, name=f"x_grp{i}") for i, (a, n) in enumerate(x_cuts)]
         x_codes = keep.tile([P, T], U32, align_bytes=64, name="x_codes")
         x_scales = keep.tile([P, T], U8, align_bytes=64, name="x_scales")
-        s_codes = keep.tile([P, SLOTS], U32, align_bytes=64, name="s_codes")
-        s_scales = keep.tile([P, SLOTS], U8, align_bytes=64, name="s_scales")
         w_raw = [keep.tile([P, PACK, N], F32, name=f"w_raw{e}") for e in range(E)]
         w_grp = [keep.tile([P, 4, P, PACK], BF16, align_bytes=64, name=f"w_grp{e}") for e in range(E)]
         w_codes = [keep.tile([P, N], U32, align_bytes=64, name=f"w_codes{e}") for e in range(E)]
@@ -84,11 +83,16 @@ def tile_moe_nxt_lin_none_kernel(tc, xT, w, wp, gate, offs, pos1, pos2, out):
                 in_=x_grp[i][:].rearrange("p t j -> p (t j)"),
             )
 
+        picked = {}
+
         def gather(e):
-            cols = slice(e * C, (e + 2) * C)
             picks = offs_sb[:, e * C // 16 : (e + 2) * C // 16]
-            nc.vector.tensor_copy(s_codes[:, cols], x_codes[:].indirect(picks))
-            nc.vector.tensor_copy(s_scales[:, cols], x_scales[:].indirect(picks))
+            codes = slots.tile([P, 2 * C], U32, align_bytes=64, name="s_codes")
+            scales = slots.tile([P, 2 * C], U8, align_bytes=64, name="s_scales")
+            nc.vector.tensor_copy(codes[:], x_codes[:].indirect(picks))
+            nc.vector.tensor_copy(scales[:], x_scales[:].indirect(picks))
+            picked[e] = (codes[:, 0:C], scales[:, 0:C])
+            picked[e + 1] = (codes[:, C : 2 * C], scales[:, C : 2 * C])
 
         def interleave_w(e):
             s = SHARES[e]
@@ -114,24 +118,46 @@ def tile_moe_nxt_lin_none_kernel(tc, xT, w, wp, gate, offs, pos1, pos2, out):
                     out=bank[r][:, col : col + C],
                     lhsT=w_codes[e][:, r * P : (r + 1) * P].bitcast(FP8X4),
                     lhsT_scale=w_scales[e][:, r * P : (r + 1) * P],
-                    rhs=s_codes[:, e * C : (e + 1) * C].bitcast(FP8X4),
-                    rhs_scale=s_scales[:, e * C : (e + 1) * C],
+                    rhs=picked[e][0].bitcast(FP8X4),
+                    rhs_scale=picked[e][1],
                     start=True,
                     stop=True,
                 )
 
+        banks = {}
+
+        def start_group(g):
+            banks[g] = [psum.tile([P, 2 * C], F32, name="bank") for r in range(4)]
+
+        def run_expert(e):
+            quantise_w(e, 2 if e == E - 1 else 1)
+            if e % 2 == 0:
+                start_group(e // 2)
+            expert(e, banks[e // 2], (e % 2) * C)
+
+        def keep_result(g, r):
+            nc.scalar.copy(y[r][:, 2 * g * C : 2 * (g + 1) * C], banks[g][r][:])
+
         gather(0)
-        for group in ((0, 1), (2, 3), (4,), (5,)):
-            bank = [psum.tile([P, 512], F32, name="bank") for r in range(4)]
-            for i, e in enumerate(group):
-                interleave_w(e)
-                if e % 2 == 0 and e + 2 < E:
-                    gather(e + 2)
-                quantise_w(e, 2 if e == E - 1 else 1)
-                expert(e, bank, i * C)
-            a, n = group[0] * C, len(group) * C
-            for r in range(4):
-                nc.scalar.copy(y[r][:, a : a + n], bank[r][:, 0:n])
+        interleave_w(0)
+        interleave_w(1)
+        gather(2)
+        run_expert(0)
+        run_expert(1)
+        interleave_w(2)
+        run_expert(2)
+        gather(4)
+        interleave_w(3)
+        for r in range(4):
+            keep_result(0, r)
+        run_expert(3)
+        interleave_w(4)
+        run_expert(4)
+        interleave_w(5)
+        run_expert(5)
+        for r in range(4):
+            keep_result(1, r)
+            keep_result(2, r)
 
         o, s = line_view(wp_grp[:], wp_raw[:])
         nc.scalar.copy(o, s)
@@ -156,11 +182,11 @@ def tile_moe_nxt_lin_none_kernel(tc, xT, w, wp, gate, offs, pos1, pos2, out):
                         MULT,
                     )
 
-        def combine_add(i, lo, hi):
+        def combine_add(i, lo, hi, r0, r1):
             nc.vector.tensor_tensor(
-                c_grp[i][:, lo:hi, :].rearrange("p (c i) r -> p c r i", i=4),
-                parts[i][0][:, :, lo:hi].rearrange("p r (c i) -> p c r i", i=4),
-                parts[i][1][:, :, lo:hi].rearrange("p r (c i) -> p c r i", i=4),
+                c_grp[i][:, lo:hi, r0:r1].rearrange("p (c i) r -> p c r i", i=4),
+                parts[i][0][:, r0:r1, lo:hi].rearrange("p r (c i) -> p c r i", i=4),
+                parts[i][1][:, r0:r1, lo:hi].rearrange("p r (c i) -> p c r i", i=4),
                 ADD,
             )
 
@@ -194,21 +220,18 @@ def tile_moe_nxt_lin_none_kernel(tc, xT, w, wp, gate, offs, pos1, pos2, out):
         nc.vector.quantize_mx(
             out=wp_codes[:].bitcast(FP8X4), scales=wp_scales[:], in_=wp_grp[:].rearrange("p m j -> p (m j)")
         )
-        for i in range(n_chunks):
-            last = i == n_chunks - 1
-            n = chunks[i][1]
-            if last:
-                h = n // 2
-                combine_add(i, 0, h)
-                combine_add(i, h, n)
-                quantise_c(i, 0, h)
-                quantise_c(i, h, n)
-                project(i, 0, h, (nc.scalar.copy, nc.scalar.copy))
-                project(i, h, n, (nc.scalar.copy, nc.vector.tensor_copy))
-            else:
-                combine_gathers(i + 1, (0, 1))
-                combine_add(i, 0, n)
-                combine_gathers(i + 1, (2, 3))
-                quantise_c(i, 0, n)
-                for lo in range(0, n, 256):
-                    project(i, lo, min(lo + 256, n), (nc.scalar.copy, nc.scalar.copy))
+        combine_gathers(1, (0,))
+        combine_add(0, 0, 512, 0, 4)
+        combine_gathers(1, (1,))
+        quantise_c(0, 0, 512)
+        project(0, 0, 256, (nc.scalar.copy, nc.scalar.copy))
+        project(0, 256, 512, (nc.scalar.copy, nc.scalar.copy))
+        combine_gathers(1, (2,))
+        combine_add(1, 0, 256, 0, 2)
+        combine_gathers(1, (3,))
+        combine_add(1, 0, 128, 2, 4)
+        combine_add(1, 128, 256, 2, 4)
+        quantise_c(1, 0, 128)
+        quantise_c(1, 128, 256)
+        project(1, 0, 128, (nc.scalar.copy, nc.vector.tensor_copy))
+        project(1, 128, 256, (nc.scalar.copy, nc.vector.tensor_copy))

@@ -21,7 +21,7 @@ COPY = mybir.ActivationFunctionType.Copy
 FLOPS = 2 * SLOTS * K * N + 2 * T * N * M
 BYTES = 4 * (K * T + E * K * N + N * M + 2 * T + M * T) + 2 * (SLOTS + 2 * T)
 
-SHARES = (128, 128, 128, 128, 112, 96)
+SHARES = ((96, 96), (96, 96), (96, 96), (112, 112), (112, 128), (72, 128))
 CHUNKS = (512, 256)
 
 
@@ -95,13 +95,18 @@ def tile_moe_nxt_lin_none_kernel(tc, xT, w, wp, gate, offs, pos1, pos2, out):
             picked[e + 1] = (codes[:, C : 2 * C], scales[:, C : 2 * C])
 
         def interleave_w(e):
-            s = SHARES[e]
-            for a, b, copy in ((0, s, nc.scalar.copy), (s, P, nc.vector.tensor_copy)):
+            s, v = SHARES[e]
+            cuts = [(0, s, 0), (s, v, 1)] + [(a, min(a + 16, P), 2) for a in range(v, P, 16)]
+            for a, b, who in cuts:
                 if a < b:
-                    copy(
-                        w_grp[e][:, :, a:b, :].rearrange("p r m j -> p m j r"),
-                        w_raw[e][:, :, 4 * a : 4 * b].rearrange("p j (m r) -> p m j r", r=4),
-                    )
+                    o = w_grp[e][:, :, a:b, :].rearrange("p r m j -> p m j r")
+                    i = w_raw[e][:, :, 4 * a : 4 * b].rearrange("p j (m r) -> p m j r", r=4)
+                    if who == 0:
+                        nc.scalar.copy(o, i)
+                    elif who == 1:
+                        nc.vector.tensor_copy(o, i)
+                    else:
+                        nc.gpsimd.tensor_scalar(o, i, 1.0, 0.0, MULT, ADD)
 
         def quantise_w(e, cuts):
             for a in range(0, 4, 4 // cuts):
@@ -112,10 +117,15 @@ def tile_moe_nxt_lin_none_kernel(tc, xT, w, wp, gate, offs, pos1, pos2, out):
                     in_=w_grp[e][:, a:b, :, :].rearrange("p r m j -> p (r m j)"),
                 )
 
-        def expert(e, bank, col):
-            for r in range(4):
+        banks = [[None] * 4 for g in range(E // 2)]
+
+        def expert(e, rows):
+            g, half = divmod(e, 2)
+            for r in rows:
+                if half == 0:
+                    banks[g][r] = psum.tile([P, 2 * C], F32, name="bank")
                 nc.tensor.matmul_mx(
-                    out=bank[r][:, col : col + C],
+                    out=banks[g][r][:, half * C : (half + 1) * C],
                     lhsT=w_codes[e][:, r * P : (r + 1) * P].bitcast(FP8X4),
                     lhsT_scale=w_scales[e][:, r * P : (r + 1) * P],
                     rhs=picked[e][0].bitcast(FP8X4),
@@ -124,38 +134,33 @@ def tile_moe_nxt_lin_none_kernel(tc, xT, w, wp, gate, offs, pos1, pos2, out):
                     stop=True,
                 )
 
-        banks = {}
-
-        def start_group(g):
-            banks[g] = [psum.tile([P, 2 * C], F32, name="bank") for r in range(4)]
-
-        def run_expert(e):
-            quantise_w(e, 2 if e == E - 1 else 1)
-            if e % 2 == 0:
-                start_group(e // 2)
-            expert(e, banks[e // 2], (e % 2) * C)
-
         def keep_result(g, r):
             nc.scalar.copy(y[r][:, 2 * g * C : 2 * (g + 1) * C], banks[g][r][:])
 
+        rows = range(4)
         gather(0)
         interleave_w(0)
         interleave_w(1)
         gather(2)
-        run_expert(0)
-        run_expert(1)
+        quantise_w(0, 1)
+        expert(0, rows)
+        quantise_w(1, 1)
+        expert(1, rows)
         interleave_w(2)
-        run_expert(2)
+        quantise_w(2, 1)
+        expert(2, rows)
         gather(4)
         interleave_w(3)
-        for r in range(4):
-            keep_result(0, r)
-        run_expert(3)
+        quantise_w(3, 1)
+        expert(3, rows)
         interleave_w(4)
-        run_expert(4)
         interleave_w(5)
-        run_expert(5)
-        for r in range(4):
+        quantise_w(4, 1)
+        quantise_w(5, 2)
+        for r in rows:
+            keep_result(0, r)
+            expert(4, (r,))
+            expert(5, (r,))
             keep_result(1, r)
             keep_result(2, r)
 

@@ -21,8 +21,9 @@ COPY = mybir.ActivationFunctionType.Copy
 FLOPS = 2 * SLOTS * K * N + 2 * T * N * M
 BYTES = 4 * (K * T + E * K * N + N * M + 2 * T + M * T) + 2 * (SLOTS + 2 * T)
 
-SHARES = ((96, 96), (96, 96), (96, 96), (112, 112), (112, 128), (72, 128))
+SHARES = ((96, 96), (80, 128), (72, 128), (72, 128), (72, 128), (56, 128))
 CHUNKS = (512, 256)
+X_VECTOR = (344, 168)
 
 
 def tile_moe_nxt_lin_none_kernel(tc, xT, w, wp, gate, offs, pos1, pos2, out):
@@ -71,7 +72,7 @@ def tile_moe_nxt_lin_none_kernel(tc, xT, w, wp, gate, offs, pos1, pos2, out):
             return (grouped.rearrange("p (c i) j -> p c j i", i=4), raw.rearrange("p j (c i) -> p c j i", i=4))
 
         for i, (a, n) in enumerate(x_cuts):
-            h = n // 2
+            h = X_VECTOR[i]
             o, s = line_view(x_grp[i][:, 0:h, :], x_raw[i][:, :, 0:h])
             nc.vector.tensor_copy(o, s)
             o, s = line_view(x_grp[i][:, h:n, :], x_raw[i][:, :, h:n])

from contextlib import ExitStack

import concourse.mybir as mybir

K, T, E, C, N, M = 512, 768, 6, 256, 512, 512
SLOTS = E * C
P = 128
PACK = 4

F32 = mybir.dt.float32
BF16 = mybir.dt.bfloat16
I32 = mybir.dt.int32
U32 = mybir.dt.uint32
U16 = mybir.dt.uint16
U8 = mybir.dt.uint8
FP8X4 = mybir.dt.float8_e4m3fn_x4
MULT = mybir.AluOpType.mult
ADD = mybir.AluOpType.add
COPY = mybir.ActivationFunctionType.Copy

FLOPS = 2 * SLOTS * K * N + 2 * T * N * M
BYTES = 4 * (K * T + E * K * N + N * M + 2 * T + M * T) + 2 * (SLOTS + 2 * T)

SHARES = ((96, 96), (80, 128), (72, 128), (72, 128), (72, 128), (56, 128))
CHUNKS = (512, 256)
X_VECTOR = (344, 168)


def tile_moe_nxt_lin_none_kernel(tc, xT, w, wp, gate, offs, pos1, pos2, out):
    nc = tc.nc
    with ExitStack() as ctx:
        lists = ctx.enter_context(tc.tile_pool(name="lists", bufs=1))
        keep = ctx.enter_context(tc.tile_pool(name="keep", bufs=1))
        slots = ctx.enter_context(tc.tile_pool(name="slots", bufs=2))
        psum = ctx.enter_context(tc.psum_pool(name="psum", bufs=8))

        offs_sb = lists.tile([P, SLOTS // 16], U16, name="offs_sb")
        pos1_sb = lists.tile([P, T // 16], U16, name="pos1_sb")
        pos2_sb = lists.tile([P, T // 16], U16, name="pos2_sb")

        x_cuts = [(0, 512), (512, 256)]
        x_view = xT.rearrange("(p j) t -> p j t", j=PACK)
        x_raw = [keep.tile([P, PACK, n], F32, name=f"x_raw{i}") for i, (a, n) in enumerate(x_cuts)]
        x_grp = [keep.tile([P, n, PACK], BF16, align_bytes=64, name=f"x_grp{i}") for i, (a, n) in enumerate(x_cuts)]
        x_codes = keep.tile([P, T], U32, align_bytes=64, name="x_codes")
        x_scales = keep.tile([P, T], U8, align_bytes=64, name="x_scales")
        w_raw = [keep.tile([P, PACK, N], F32, name=f"w_raw{e}") for e in range(E)]
        w_grp = [keep.tile([P, 4, P, PACK], BF16, align_bytes=64, name=f"w_grp{e}") for e in range(E)]
        w_codes = [keep.tile([P, N], U32, align_bytes=64, name=f"w_codes{e}") for e in range(E)]
        w_scales = [keep.tile([P, N], U8, align_bytes=64, name=f"w_scales{e}") for e in range(E)]
        wp_raw = keep.tile([P, PACK, M], F32, name="wp_raw")
        wp_grp = keep.tile([P, M, PACK], BF16, align_bytes=64, name="wp_grp")
        wp_codes = keep.tile([P, M], U32, align_bytes=64, name="wp_codes")
        wp_scales = keep.tile([P, M], U8, align_bytes=64, name="wp_scales")
        gate_sb = keep.tile([P, 2, T], F32, name="gate_sb")
        y = [keep.tile([P, SLOTS], F32, name=f"y{r}") for r in range(4)]

        for i, (a, n) in enumerate(x_cuts):
            nc.sync.dma_start(x_raw[i][:], x_view[:, :, a : a + n])
            if i == 0:
                nc.sync.dma_start(offs_sb[:], offs)
        for e in range(E):
            nc.sync.dma_start(w_raw[e][:], w[e].rearrange("(p j) n -> p j n", j=PACK))
        nc.sync.dma_start(pos1_sb[:], pos1)
        nc.sync.dma_start(pos2_sb[:], pos2)
        nc.sync.dma_start(gate_sb[:], gate[:, 0:P, :].rearrange("g p t -> p g t"))
        nc.sync.dma_start(wp_raw[:], wp.rearrange("(p j) m -> p j m", j=PACK))

        nc.gpsimd.memset(x_scales[:], 0)

        def line_view(grouped, raw):
            return (grouped.rearrange("p (c i) j -> p c j i", i=4), raw.rearrange("p j (c i) -> p c j i", i=4))

        for i, (a, n) in enumerate(x_cuts):
            h = X_VECTOR[i]
            o, s = line_view(x_grp[i][:, 0:h, :], x_raw[i][:, :, 0:h])
            nc.vector.tensor_copy(o, s)
            o, s = line_view(x_grp[i][:, h:n, :], x_raw[i][:, :, h:n])
            nc.scalar.activation(o, s, COPY)
        for i, (a, n) in enumerate(x_cuts):
            nc.vector.quantize_mx(
                out=x_codes[:, a : a + n].bitcast(FP8X4),
                scales=x_scales[:, a : a + n],
                in_=x_grp[i][:].rearrange("p t j -> p (t j)"),
            )

        picked = {}

        def gather(e):
            picks = offs_sb[:, e * C // 16 : (e + 2) * C // 16]
            codes = slots.tile([P, 2 * C], U32, align_bytes=64, name="s_codes")
            scales = slots.tile([P, 2 * C], U8, align_bytes=64, name="s_scales")
            nc.vector.tensor_copy(codes[:], x_codes[:].indirect(picks))
            nc.vector.tensor_copy(scales[:], x_scales[:].indirect(picks))
            picked[e] = (codes[:, 0:C], scales[:, 0:C])
            picked[e + 1] = (codes[:, C : 2 * C], scales[:, C : 2 * C])

        def interleave_w(e):
            s, v = SHARES[e]
            cuts = [(0, s, 0), (s, v, 1)] + [(a, min(a + 16, P), 2) for a in range(v, P, 16)]
            for a, b, who in cuts:
                if a < b:
                    o = w_grp[e][:, :, a:b, :].rearrange("p r m j -> p m j r")
                    i = w_raw[e][:, :, 4 * a : 4 * b].rearrange("p j (m r) -> p m j r", r=4)
                    if who == 0:
                        nc.scalar.copy(o, i)
                    elif who == 1:
                        nc.vector.tensor_copy(o, i)
                    else:
                        nc.gpsimd.tensor_scalar(o, i, 1.0, 0.0, MULT, ADD)

        def quantise_w(e, cuts):
            for a in range(0, 4, 4 // cuts):
                b = a + 4 // cuts
                nc.vector.quantize_mx(
                    out=w_codes[e][:, a * P : b * P].bitcast(FP8X4),
                    scales=w_scales[e][:, a * P : b * P],
                    in_=w_grp[e][:, a:b, :, :].rearrange("p r m j -> p (r m j)"),
                )

        banks = [[None] * 4 for g in range(E // 2)]

        def expert(e, rows):
            g, half = divmod(e, 2)
            for r in rows:
                if half == 0:
                    banks[g][r] = psum.tile([P, 2 * C], F32, name="bank")
                nc.tensor.matmul_mx(
                    out=banks[g][r][:, half * C : (half + 1) * C],
                    lhsT=w_codes[e][:, r * P : (r + 1) * P].bitcast(FP8X4),
                    lhsT_scale=w_scales[e][:, r * P : (r + 1) * P],
                    rhs=picked[e][0].bitcast(FP8X4),
                    rhs_scale=picked[e][1],
                    start=True,
                    stop=True,
                )

        def keep_result(g, r):
            nc.scalar.copy(y[r][:, 2 * g * C : 2 * (g + 1) * C], banks[g][r][:])

        rows = range(4)
        gather(0)
        interleave_w(0)
        interleave_w(1)
        gather(2)
        quantise_w(0, 1)
        expert(0, rows)
        quantise_w(1, 1)
        expert(1, rows)
        interleave_w(2)
        quantise_w(2, 1)
        expert(2, rows)
        gather(4)
        interleave_w(3)
        quantise_w(3, 1)
        expert(3, rows)
        interleave_w(4)
        interleave_w(5)
        quantise_w(4, 1)
        quantise_w(5, 2)
        for r in rows:
            keep_result(0, r)
            expert(4, (r,))
            expert(5, (r,))
            keep_result(1, r)
            keep_result(2, r)

        o, s = line_view(wp_grp[:], wp_raw[:])
        nc.scalar.copy(o, s)

        chunks = [(sum(CHUNKS[:i]), n) for i, n in enumerate(CHUNKS)]
        n_chunks = len(chunks)
        parts = [[keep.tile([P, 4, n], F32, name=f"part{q}_{i}") for q in range(2)] for i, (a, n) in enumerate(chunks)]
        c_grp = [keep.tile([P, n, 4], BF16, align_bytes=64, name=f"c_grp{i}") for i, (a, n) in enumerate(chunks)]
        c_codes = [keep.tile([P, n], U32, align_bytes=64, name=f"c_codes{i}") for i, (a, n) in enumerate(chunks)]
        c_scales = [keep.tile([P, n], U8, align_bytes=64, name=f"c_scales{i}") for i, (a, n) in enumerate(chunks)]
        o_sb = [keep.tile([P, 4, n], F32, name=f"o_sb{i}") for i, (a, n) in enumerate(chunks)]
        out_view = out.rearrange("(f p) t -> p f t", p=P)

        def combine_gathers(i, rows):
            a, n = chunks[i]
            for r in rows:
                for q, pos in enumerate((pos1_sb, pos2_sb)):
                    nc.vector.tensor_tensor(
                        parts[i][q][:, r, :],
                        y[r][:].indirect(pos[:, a // 16 : (a + n) // 16]),
                        gate_sb[:, q, a : a + n],
                        MULT,
                    )

        def combine_add(i, lo, hi, r0, r1):
            nc.vector.tensor_tensor(
                c_grp[i][:, lo:hi, r0:r1].rearrange("p (c i) r -> p c r i", i=4),
                parts[i][0][:, r0:r1, lo:hi].rearrange("p r (c i) -> p c r i", i=4),
                parts[i][1][:, r0:r1, lo:hi].rearrange("p r (c i) -> p c r i", i=4),
                ADD,
            )

        def quantise_c(i, lo, hi):
            nc.vector.quantize_mx(
                out=c_codes[i][:, lo:hi].bitcast(FP8X4),
                scales=c_scales[i][:, lo:hi],
                in_=c_grp[i][:, lo:hi, :].rearrange("p t r -> p (t r)"),
            )

        def project(i, lo, hi, engines):
            a, n = chunks[i]
            w_cols = hi - lo
            for half in range(2):
                bank = psum.tile([P, 2, w_cols], F32, name="bank")
                for u in range(2):
                    f = 2 * half + u
                    nc.tensor.matmul_mx(
                        out=bank[:, u, :],
                        lhsT=wp_codes[:, f * P : (f + 1) * P].bitcast(FP8X4),
                        lhsT_scale=wp_scales[:, f * P : (f + 1) * P],
                        rhs=c_codes[i][:, lo:hi].bitcast(FP8X4),
                        rhs_scale=c_scales[i][:, lo:hi],
                        start=True,
                        stop=True,
                    )
                engines[half](o_sb[i][:, 2 * half : 2 * half + 2, lo:hi], bank[:])
            nc.sync.dma_start(out_view[:, :, a + lo : a + hi], o_sb[i][:, :, lo:hi])

        combine_gathers(0, (0, 1, 2, 3))
        nc.vector.quantize_mx(
            out=wp_codes[:].bitcast(FP8X4), scales=wp_scales[:], in_=wp_grp[:].rearrange("p m j -> p (m j)")
        )
        combine_gathers(1, (0,))
        combine_add(0, 0, 512, 0, 4)
        combine_gathers(1, (1,))
        quantise_c(0, 0, 512)
        project(0, 0, 256, (nc.scalar.copy, nc.scalar.copy))
        project(0, 256, 512, (nc.scalar.copy, nc.scalar.copy))
        combine_gathers(1, (2,))
        combine_add(1, 0, 256, 0, 2)
        combine_gathers(1, (3,))
        combine_add(1, 0, 128, 2, 4)
        combine_add(1, 128, 256, 2, 4)
        quantise_c(1, 0, 128)
        quantise_c(1, 128, 256)
        project(1, 0, 128, (nc.scalar.copy, nc.vector.tensor_copy))
        project(1, 128, 256, (nc.scalar.copy, nc.vector.tensor_copy))
